import numpy as np
import ml_dtypes


def mxq(x, axis, fmt="e4m3"):
    dtype, down = {"e4m3": (ml_dtypes.float8_e4m3fn, 7), "e5m2": (ml_dtypes.float8_e5m2, 14)}[fmt]
    v = np.moveaxis(np.asarray(x, np.float32).astype(ml_dtypes.bfloat16).astype(np.float64), axis, -1)
    blocks = v.reshape(v.shape[:-1] + (-1, 32))
    amax = np.abs(blocks).max(-1, keepdims=True)
    byte = np.maximum(np.where(amax > 0, np.frexp(amax)[1] - 1 + 127, 0) - down, 1)
    scale = np.exp2(byte - 127.0)
    codes = (blocks / scale).astype(np.float32).astype(dtype).astype(np.float64)
    return np.moveaxis((codes * scale).reshape(v.shape), -1, axis)


WIDE = False


def mx_kscale(k):
    if not WIDE:
        return np.ones(k)
    levels = np.array([10, -10, 5, -5, 0])
    if k % 512:
        return np.exp2(np.random.permutation(np.resize(levels, k // 32))).repeat(32)
    a = np.empty((k // 512, 16))
    for p in range(k // 512):
        a[p, :8] = np.random.permutation(np.resize(levels, 8))
        for g in range(8):
            far = levels[np.abs(levels - a[p, g]) >= 10]
            a[p, g + 8] = far[np.random.randint(len(far))]
    return np.exp2(a.ravel()).repeat(32)


def f64(x):
    return np.asarray(x).astype(np.float64)


def striped(idx):
    return np.tile(idx.reshape(-1, 16).T, (8, 1)).astype(np.uint16)


def unstriped(offs):
    return offs[:16].T.reshape(-1).astype(np.int64)


def pack_weight(w):
    k, n = w.shape
    w = f64(np.asarray(w, np.float32).astype(ml_dtypes.bfloat16)).reshape(k // 32, 32, n)
    amax = np.abs(w).max(1)
    byte = np.clip(np.where(amax > 0, np.frexp(amax)[1] - 1 + 127 - 7, 1), 1, 254)
    scaled = (w * np.exp2(127.0 - byte)[:, None, :]).reshape(k, n).astype(np.float32)
    words = np.ascontiguousarray(scaled.reshape(k // 512, 128, 4, n).transpose(0, 1, 3, 2)).astype(ml_dtypes.float8_e4m3fn).view(np.uint8)
    return words, np.ascontiguousarray(byte.astype(np.uint8).reshape(k // 512, 16, n))


def unpack_weight(words, scales):
    g, p, n, _ = words.shape
    vals = np.ascontiguousarray(words).view(ml_dtypes.float8_e4m3fn).astype(np.float64) * np.repeat(np.exp2(scales.astype(np.float64) - 127.0), 8, axis=1)[..., None]
    return vals.transpose(0, 1, 3, 2).reshape(g * 512, n)


def relu(v):
    return np.maximum(v, 0.0)


K, T, E, C, N = 1024, 512, 4, 256, 256


def by_expert(wq, xq):
    return np.concatenate([wq[e].T @ xq[:, e * C:(e + 1) * C] for e in range(E)], axis=1)


def setup_inputs():
    n = np.random.standard_normal
    s = mx_kscale(K)[:, None]
    first = np.random.permutation(np.repeat(np.arange(E), T // E))
    second = (first + 1 + np.random.permutation(np.repeat(np.arange(E - 1), -(-T // (E - 1)))[:T])) % E
    while np.bincount(second, minlength=E).max() != T // E:
        load = np.bincount(second, minlength=E); hi, lo = int(load.argmax()), int(load.argmin())
        t = np.flatnonzero((second == hi) & (first != lo))[0]; second[t] = lo
    slot_token = np.empty(E * C, np.int64); pos = np.empty((2, T), np.int64); fill = np.zeros(E, np.int64)
    place = np.stack([np.random.permutation(C) for _ in range(E)])
    for r, deal in enumerate((first, second)):
        for t in np.random.permutation(T):
            e = deal[t]; j = e * C + place[e, fill[e]]; fill[e] += 1; slot_token[j] = t; pos[r, t] = j
    g = np.random.uniform(0.2, 0.8, T)
    packed = [pack_weight(m) for m in n((E, K, N)) / np.sqrt(K) / s[None]]
    return {
        "xT": (n((K, T)) * s).astype(np.float32),
        "w_words": np.stack([m[0] for m in packed]),
        "w_scales": np.stack([m[1] for m in packed]),
        "b": (0.3 * n((N, E))).astype(np.float32),
        "gate": np.stack([np.tile(g, (N, 1)), np.tile(1.0 - g, (N, 1))]).astype(np.float32),
        "offs": striped(slot_token),
        "pos1": striped(pos[0]),
        "pos2": striped(pos[1]),
    }


def reference(xT, w_words, w_scales, b, gate, offs, pos1, pos2):
    idx = unstriped(offs)
    xq = mxq(f64(xT)[:, idx], 0, "e4m3")
    w = np.stack([unpack_weight(w_words[e], w_scales[e]) for e in range(E)])
    y = by_expert(w, xq)
    y = relu(y + np.repeat(f64(b), C, axis=1))
    return f64(gate[0]) * y[:, unstriped(pos1)] + f64(gate[1]) * y[:, unstriped(pos2)]

@@ -1,0 +1,145 @@
+from contextlib import ExitStack
+
+import concourse.mybir as mybir
+from concourse.masks import make_identity
+
+F32 = mybir.dt.float32
+BF16 = mybir.dt.bfloat16
+U32 = mybir.dt.uint32
+I32 = mybir.dt.int32
+U16 = mybir.dt.uint16
+U8 = mybir.dt.uint8
+FP8X4 = mybir.dt.float8_e4m3fn_x4
+RELU = mybir.ActivationFunctionType.Relu
+MULT = mybir.AluOpType.mult
+ADD = mybir.AluOpType.add
+
+P = 128
+K, T, E, C, N = 1024, 512, 4, 256, 256
+G = K // 512
+NB = N // P
+S = E * C
+HALF = T // 2
+VEC = 160
+PIECES = ((0, 384), (384, 768), (768, 1024))
+
+FLOPS = 2 * K * N * S
+
+
+def tile_routed_moe_kernel(tc, xT, w_words, w_scales, b, gate, offs, pos1, pos2, out):
+    nc = tc.nc
+    with ExitStack() as ctx:
+        lists = ctx.enter_context(tc.tile_pool(name="lists", bufs=1))
+        keep = ctx.enter_context(tc.tile_pool(name="keep", bufs=1))
+        psum = ctx.enter_context(tc.psum_pool(name="psum", bufs=1))
+
+        offs_t = lists.tile([P, S // 16], U16, name="offs_t")
+        pos1_t = lists.tile([P, T // 16], U16, name="pos1_t")
+        pos2_t = lists.tile([P, T // 16], U16, name="pos2_t")
+
+        raw = [keep.tile([P, 4, T], F32, name=f"raw{g}") for g in range(G)]
+        grouped = [keep.tile([P, T, 4], BF16, name=f"grouped{g}", align_bytes=64) for g in range(G)]
+        x_words = [keep.tile([P, T], U32, name=f"x_words{g}", align_bytes=64) for g in range(G)]
+        x_scales = keep.tile([P, T], U8, name="x_scales", align_bytes=64)
+        s_words = [keep.tile([P, S], U32, name=f"s_words{g}", align_bytes=64) for g in range(G)]
+        s_scales = keep.tile([P, S], U8, name="s_scales", align_bytes=64)
+        w_codes = keep.tile([P, E * G, 4 * N], U8, name="w_codes", align_bytes=64)
+        w_planes = keep.tile([P, E * G, N], U8, name="w_planes", align_bytes=64)
+        bias = keep.tile([P, NB, E], F32, name="bias")
+        gates = keep.tile([P, NB, 2, T], F32, name="gates")
+
+        ident = keep.tile([P, P], F32, name="ident")
+        nc.gpsimd.memset(x_scales[:], 0)
+        make_identity(nc, ident[:])
+        nc.vector.memset(w_planes[:].rearrange("p a n -> p (a n)").bitcast(I32), 0)
+
+        x_view = xT.rearrange("(g p t) n -> g p t n", p=P, t=4)
+        for g in range(G):
+            for h in range(2):
+                cols = slice(h * HALF, (h + 1) * HALF)
+                nc.sync.dma_start(out=raw[g][:, :, cols], in_=x_view[g, :, :, cols])
+                if g == 0 and h == 0:
+                    nc.sync.dma_start(offs_t[:], offs)
+        nc.sync.dma_start(out=bias[:], in_=b.rearrange("(a p) e -> p a e", p=P))
+        for q in range(4):
+            nc.sync.dma_start(
+                out=w_planes[32 * q : 32 * q + 4, :, :].bitcast(I32),
+                in_=w_scales[:, :, 4 * q : 4 * q + 4, :].rearrange("e a i n -> i (e a) n").bitcast(I32),
+            )
+        w_view = w_words.rearrange("e a p n r -> p (e a) (n r)")
+        for e in range(0, E, 2):
+            ea = slice(e * G, (e + 2) * G)
+            nc.sync.dma_start(out=w_codes[:, ea, :].bitcast(I32), in_=w_view[:, ea, :].bitcast(I32))
+        nc.sync.dma_start(pos1_t[:], pos1)
+        nc.sync.dma_start(pos2_t[:], pos2)
+        for a in range(NB):
+            nc.sync.dma_start(out=gates[:, a, :, :], in_=gate[:, a * P : (a + 1) * P, :].rearrange("r p t -> p r t"))
+
+        def interleave(g, h):
+            lo, mid, hi = h * HALF, h * HALF + (VEC if g == 0 else 0), (h + 1) * HALF
+            if mid > lo:
+                nc.vector.tensor_copy(out=grouped[g][:, lo:mid, :], in_=raw[g][:, :, lo:mid].rearrange("p t n -> p n t"))
+            nc.scalar.copy(grouped[g][:, mid:hi, :], raw[g][:, :, mid:hi].rearrange("p t n -> p n t"))
+
+        def quantize(g, lo, hi):
+            cols = slice(lo, hi)
+            nc.vector.quantize_mx(
+                out=x_words[g][:, cols].bitcast(FP8X4),
+                scales=x_scales[4 * g : P, cols],
+                in_=grouped[g][:, cols, :].rearrange("p n t -> p (n t)"),
+            )
+
+        def gather(dst, src, lo, hi):
+            nc.vector.tensor_copy(dst[:, lo:hi], src[:].indirect(offs_t[:, lo // 16 : hi // 16]))
+
+        interleave(0, 0)
+        interleave(0, 1)
+        quantize(0, 0, HALF)
+        quantize(0, HALF, T)
+        interleave(1, 0)
+        interleave(1, 1)
+        for lo, hi in PIECES:
+            gather(s_words[0], x_words[0], lo, hi)
+        quantize(1, 0, T)
+        for lo, hi in PIECES:
+            gather(s_scales, x_scales, lo, hi)
+        for lo, hi in PIECES:
+            gather(s_words[1], x_words[1], lo, hi)
+
+        y = [keep.tile([P, S], F32, name=f"y{a}") for a in range(NB)]
+        for e in range(E):
+            slots = slice(e * C, (e + 1) * C)
+            for a in range(NB):
+                acc = psum.tile([P, C], F32, name=f"acc{(e * NB + a) % 7}")
+                for g in range(G):
+                    nc.tensor.matmul_mx(
+                        out=acc[:],
+                        lhsT=w_codes[:, e * G + g, a * 4 * P : (a + 1) * 4 * P].bitcast(FP8X4),
+                        lhsT_scale=w_planes[:, e * G + g, a * P : (a + 1) * P],
+                        rhs=s_words[g][:, slots].bitcast(FP8X4),
+                        rhs_scale=s_scales[4 * g : P, slots],
+                        start=(g == 0),
+                        stop=(g == G - 1),
+                    )
+                nc.scalar.activation(y[a][:, slots], acc[:], RELU, bias=bias[:, a, e : e + 1])
+
+
+        first = [keep.tile([P, T], F32, name=f"first{a}") for a in range(NB)]
+        second = [keep.tile([P, T], F32, name=f"second{a}") for a in range(NB)]
+        total = [keep.tile([P, T], F32, name=f"total{a}") for a in range(NB)]
+        both = psum.tile([P, T], F32, name="both")
+
+        nc.vector.tensor_tensor(first[0][:], y[0][:].indirect(pos1_t[:]), gates[:, 0, 0, :], MULT)
+        nc.tensor.matmul(both[:], ident[:], first[0][:], start=True, stop=False)
+        nc.vector.tensor_tensor(second[0][:], y[0][:].indirect(pos2_t[:]), gates[:, 0, 1, :], MULT)
+        nc.tensor.matmul(both[:], ident[:], second[0][:], start=False, stop=True)
+        nc.scalar.copy(total[0][:], both[:])
+        nc.sync.dma_start(out=out[:P, :], in_=total[0][:])
+        nc.vector.tensor_tensor(first[1][:], y[1][:].indirect(pos1_t[:]), gates[:, 1, 0, :], MULT)
+        for h in range(2):
+            cols = slice(h * HALF, (h + 1) * HALF)
+            nc.vector.tensor_tensor(second[1][:, cols], y[1][:].indirect(pos2_t[:, h * 16 : (h + 1) * 16]), gates[:, 1, 1, cols], MULT)
+        for h in range(2):
+            cols = slice(h * HALF, (h + 1) * HALF)
+            nc.vector.tensor_tensor(total[1][:, cols], first[1][:, cols], second[1][:, cols], ADD)
+            nc.sync.dma_start(out=out[P:, cols], in_=total[1][:, cols])

@@ -20,7 +20,9 @@ G = K // 512
 NB = N // P
 S = E * C
 HALF = T // 2
-VEC = 160
+LOADS = (((0, 384), (384, 512)), ((0, 256), (256, 512)))
+VEC = {0: 248, 384: 84}
+SPLIT = 224
 PIECES = ((0, 384), (384, 768), (768, 1024))
 
 FLOPS = 2 * K * N * S
@@ -55,12 +57,10 @@ def tile_routed_moe_kernel(tc, xT, w_words, w_scales, b, gate, offs, pos1, pos2,
 
         x_view = xT.rearrange("(g p t) n -> g p t n", p=P, t=4)
         for g in range(G):
-            for h in range(2):
-                cols = slice(h * HALF, (h + 1) * HALF)
-                nc.sync.dma_start(out=raw[g][:, :, cols], in_=x_view[g, :, :, cols])
-                if g == 0 and h == 0:
-                    nc.sync.dma_start(offs_t[:], offs)
-        nc.sync.dma_start(out=bias[:], in_=b.rearrange("(a p) e -> p a e", p=P))
+            for lo, hi in LOADS[g]:
+                nc.sync.dma_start(out=raw[g][:, :, lo:hi], in_=x_view[g, :, :, lo:hi])
+            if g == 0:
+                nc.sync.dma_start(offs_t[:], offs)
         for q in range(4):
             nc.sync.dma_start(
                 out=w_planes[32 * q : 32 * q + 4, :, :].bitcast(I32),
@@ -70,16 +70,20 @@ def tile_routed_moe_kernel(tc, xT, w_words, w_scales, b, gate, offs, pos1, pos2,
         for e in range(0, E, 2):
             ea = slice(e * G, (e + 2) * G)
             nc.sync.dma_start(out=w_codes[:, ea, :].bitcast(I32), in_=w_view[:, ea, :].bitcast(I32))
+        nc.sync.dma_start(out=bias[:], in_=b.rearrange("(a p) e -> p a e", p=P))
         nc.sync.dma_start(pos1_t[:], pos1)
         nc.sync.dma_start(pos2_t[:], pos2)
         for a in range(NB):
             nc.sync.dma_start(out=gates[:, a, :, :], in_=gate[:, a * P : (a + 1) * P, :].rearrange("r p t -> p r t"))
 
-        def interleave(g, h):
-            lo, mid, hi = h * HALF, h * HALF + (VEC if g == 0 else 0), (h + 1) * HALF
-            if mid > lo:
-                nc.vector.tensor_copy(out=grouped[g][:, lo:mid, :], in_=raw[g][:, :, lo:mid].rearrange("p t n -> p n t"))
-            nc.scalar.copy(grouped[g][:, mid:hi, :], raw[g][:, :, mid:hi].rearrange("p t n -> p n t"))
+        def interleave(g, lo, hi):
+            mid = lo + VEC[lo] if g == 0 else lo
+            for engine_copy, a, z in ((nc.vector.tensor_copy, lo, mid), (nc.scalar.copy, mid, hi)):
+                if z > a:
+                    engine_copy(
+                        grouped[g][:, a:z, :].rearrange("p (c i) t -> p c t i", i=4),
+                        raw[g][:, :, a:z].rearrange("p t (c i) -> p c t i", i=4),
+                    )
 
         def quantize(g, lo, hi):
             cols = slice(lo, hi)
@@ -92,54 +96,69 @@ def tile_routed_moe_kernel(tc, xT, w_words, w_scales, b, gate, offs, pos1, pos2,
         def gather(dst, src, lo, hi):
             nc.vector.tensor_copy(dst[:, lo:hi], src[:].indirect(offs_t[:, lo // 16 : hi // 16]))
 
-        interleave(0, 0)
-        interleave(0, 1)
-        quantize(0, 0, HALF)
-        quantize(0, HALF, T)
-        interleave(1, 0)
-        interleave(1, 1)
+        for lo, hi in LOADS[0]:
+            interleave(0, lo, hi)
+        quantize(0, 0, 256)
+        quantize(0, 256, 384)
+        quantize(0, 384, 512)
+        for lo, hi in LOADS[1]:
+            interleave(1, lo, hi)
         for lo, hi in PIECES:
             gather(s_words[0], x_words[0], lo, hi)
         quantize(1, 0, T)
         for lo, hi in PIECES:
             gather(s_scales, x_scales, lo, hi)
-        for lo, hi in PIECES:
-            gather(s_words[1], x_words[1], lo, hi)
+        for e in range(E):
+            gather(s_words[1], x_words[1], e * C, (e + 1) * C)
 
         y = [keep.tile([P, S], F32, name=f"y{a}") for a in range(NB)]
-        for e in range(E):
+        acc = {}
+
+        def multiply(g, e, a):
             slots = slice(e * C, (e + 1) * C)
+            if g == 0:
+                acc[e, a] = psum.tile([P, C], F32, name=f"acc{e}_{a}")
+            nc.tensor.matmul_mx(
+                out=acc[e, a][:],
+                lhsT=w_codes[:, e * G + g, a * 4 * P : (a + 1) * 4 * P].bitcast(FP8X4),
+                lhsT_scale=w_planes[:, e * G + g, a * P : (a + 1) * P],
+                rhs=s_words[g][:, slots].bitcast(FP8X4),
+                rhs_scale=s_scales[4 * g : P, slots],
+                start=(g == 0),
+                stop=(g == G - 1),
+            )
+
+        for e in range(E):
             for a in range(NB):
-                acc = psum.tile([P, C], F32, name=f"acc{(e * NB + a) % 7}")
-                for g in range(G):
-                    nc.tensor.matmul_mx(
-                        out=acc[:],
-                        lhsT=w_codes[:, e * G + g, a * 4 * P : (a + 1) * 4 * P].bitcast(FP8X4),
-                        lhsT_scale=w_planes[:, e * G + g, a * P : (a + 1) * P],
-                        rhs=s_words[g][:, slots].bitcast(FP8X4),
-                        rhs_scale=s_scales[4 * g : P, slots],
-                        start=(g == 0),
-                        stop=(g == G - 1),
-                    )
-                nc.scalar.activation(y[a][:, slots], acc[:], RELU, bias=bias[:, a, e : e + 1])
+                multiply(0, e, a)
+        for a in range(NB):
+            for e in range(E):
+                multiply(1, e, a)
+                slots = slice(e * C, (e + 1) * C)
+                nc.scalar.activation(y[a][:, slots], acc[e, a][:], RELU, bias=bias[:, a, e : e + 1])
 
-
-        first = [keep.tile([P, T], F32, name=f"first{a}") for a in range(NB)]
+        first = [keep.tile([P, T], F32, name="first0"), None]
         second = [keep.tile([P, T], F32, name=f"second{a}") for a in range(NB)]
         total = [keep.tile([P, T], F32, name=f"total{a}") for a in range(NB)]
-        both = psum.tile([P, T], F32, name="both")
+        both = [psum.tile([P, T], F32, name=f"acc{a}_0") for a in range(NB)]
 
-        nc.vector.tensor_tensor(first[0][:], y[0][:].indirect(pos1_t[:]), gates[:, 0, 0, :], MULT)
-        nc.tensor.matmul(both[:], ident[:], first[0][:], start=True, stop=False)
-        nc.vector.tensor_tensor(second[0][:], y[0][:].indirect(pos2_t[:]), gates[:, 0, 1, :], MULT)
-        nc.tensor.matmul(both[:], ident[:], second[0][:], start=False, stop=True)
-        nc.scalar.copy(total[0][:], both[:])
-        nc.sync.dma_start(out=out[:P, :], in_=total[0][:])
-        nc.vector.tensor_tensor(first[1][:], y[1][:].indirect(pos1_t[:]), gates[:, 1, 0, :], MULT)
-        for h in range(2):
-            cols = slice(h * HALF, (h + 1) * HALF)
-            nc.vector.tensor_tensor(second[1][:, cols], y[1][:].indirect(pos2_t[:, h * 16 : (h + 1) * 16]), gates[:, 1, 1, cols], MULT)
-        for h in range(2):
-            cols = slice(h * HALF, (h + 1) * HALF)
-            nc.vector.tensor_tensor(total[1][:, cols], first[1][:, cols], second[1][:, cols], ADD)
-            nc.sync.dma_start(out=out[P:, cols], in_=total[1][:, cols])
+        def fetch(dst, a, r, lo, hi):
+            pos_t = (pos1_t, pos2_t)[r]
+            nc.vector.tensor_tensor(dst[:, lo:hi], y[a][:].indirect(pos_t[:, lo // 16 : hi // 16]), gates[:, a, r, lo:hi], MULT)
+
+        def add_on_tensor(a, hi):
+            nc.tensor.matmul(both[a][:, :hi], ident[:], first[a][:, :hi], start=True, stop=False)
+            nc.tensor.matmul(both[a][:, :hi], ident[:], second[a][:, :hi], start=False, stop=True)
+            nc.scalar.copy(total[a][:, :hi], both[a][:, :hi])
+            nc.sync.dma_start(out=out[a * P : (a + 1) * P, :hi], in_=total[a][:, :hi])
+
+        fetch(first[0], 0, 0, 0, T)
+        fetch(second[0], 0, 1, 0, T)
+        add_on_tensor(0, T)
+        first[1] = keep.tile([P, T], F32, name="y0")
+        fetch(first[1], 1, 0, 0, T)
+        fetch(second[1], 1, 1, 0, SPLIT)
+        add_on_tensor(1, SPLIT)
+        fetch(second[1], 1, 1, SPLIT, T)
+        nc.vector.tensor_tensor(total[1][:, SPLIT:], first[1][:, SPLIT:], second[1][:, SPLIT:], ADD)
+        nc.sync.dma_start(out=out[P:, SPLIT:], in_=total[1][:, SPLIT:])

@@ -22,7 +22,8 @@ S = E * C
 HALF = T // 2
 LOADS = (((0, 384), (384, 512)), ((0, 256), (256, 512)))
 VEC = {0: 248, 384: 84}
-SPLIT = 224
+BY_PE = 384
+SPLIT = 320
 PIECES = ((0, 384), (384, 768), (768, 1024))
 
 FLOPS = 2 * K * N * S
@@ -111,7 +112,7 @@ def tile_routed_moe_kernel(tc, xT, w_words, w_scales, b, gate, offs, pos1, pos2,
         for e in range(E):
             gather(s_words[1], x_words[1], e * C, (e + 1) * C)
 
-        y = [keep.tile([P, S], F32, name=f"y{a}") for a in range(NB)]
+        y = [keep.tile([P, S], F32, name=name, align_bytes=64) for name in ("y0", "s_words1")]
         acc = {}
 
         def multiply(g, e, a):
@@ -140,25 +141,26 @@ def tile_routed_moe_kernel(tc, xT, w_words, w_scales, b, gate, offs, pos1, pos2,
         first = [keep.tile([P, T], F32, name="first0"), None]
         second = [keep.tile([P, T], F32, name=f"second{a}") for a in range(NB)]
         total = [keep.tile([P, T], F32, name=f"total{a}") for a in range(NB)]
-        both = [psum.tile([P, T], F32, name=f"acc{a}_0") for a in range(NB)]
+        both = psum.tile([P, T], F32, name="acc0_0")
 
         def fetch(dst, a, r, lo, hi):
             pos_t = (pos1_t, pos2_t)[r]
             nc.vector.tensor_tensor(dst[:, lo:hi], y[a][:].indirect(pos_t[:, lo // 16 : hi // 16]), gates[:, a, r, lo:hi], MULT)
 
-        def add_on_tensor(a, hi):
-            nc.tensor.matmul(both[a][:, :hi], ident[:], first[a][:, :hi], start=True, stop=False)
-            nc.tensor.matmul(both[a][:, :hi], ident[:], second[a][:, :hi], start=False, stop=True)
-            nc.scalar.copy(total[a][:, :hi], both[a][:, :hi])
-            nc.sync.dma_start(out=out[a * P : (a + 1) * P, :hi], in_=total[a][:, :hi])
+        def add_on_vector(a, lo, hi):
+            nc.vector.tensor_tensor(total[a][:, lo:hi], first[a][:, lo:hi], second[a][:, lo:hi], ADD)
+            nc.sync.dma_start(out=out[a * P : (a + 1) * P, lo:hi], in_=total[a][:, lo:hi])
 
         fetch(first[0], 0, 0, 0, T)
+        nc.tensor.matmul(both[:, :BY_PE], ident[:], first[0][:, :BY_PE], start=True, stop=False)
         fetch(second[0], 0, 1, 0, T)
-        add_on_tensor(0, T)
-        first[1] = keep.tile([P, T], F32, name="y0")
+        nc.tensor.matmul(both[:, :BY_PE], ident[:], second[0][:, :BY_PE], start=False, stop=True)
+        nc.scalar.copy(total[0][:, :BY_PE], both[:, :BY_PE])
+        nc.sync.dma_start(out=out[:P, :BY_PE], in_=total[0][:, :BY_PE])
+        first[1] = keep.tile([P, T], F32, name="y0", align_bytes=64)
         fetch(first[1], 1, 0, 0, T)
-        fetch(second[1], 1, 1, 0, SPLIT)
-        add_on_tensor(1, SPLIT)
-        fetch(second[1], 1, 1, SPLIT, T)
-        nc.vector.tensor_tensor(total[1][:, SPLIT:], first[1][:, SPLIT:], second[1][:, SPLIT:], ADD)
-        nc.sync.dma_start(out=out[P:, SPLIT:], in_=total[1][:, SPLIT:])
+        add_on_vector(0, BY_PE, T)
+        for lo, hi in ((0, SPLIT), (SPLIT, T)):
+            fetch(second[1], 1, 1, lo, hi)
+        for lo, hi in ((0, SPLIT), (SPLIT, T)):
+            add_on_vector(1, lo, hi)

@@ -20,10 +20,11 @@ G = K // 512
 NB = N // P
 S = E * C
 HALF = T // 2
-LOADS = (((0, 384), (384, 512)), ((0, 256), (256, 512)))
+LOADS = (((0, 384), (384, 512)), ((0, 192), (192, 384), (384, 512)))
 VEC = {0: 248, 384: 84}
 BY_PE = 384
 SPLIT = 320
+RUNS = ((0, 256), (256, 512), (512, 768), (768, 896), (896, 1024))
 PIECES = ((0, 384), (384, 768), (768, 1024))
 
 FLOPS = 2 * K * N * S
@@ -109,39 +110,42 @@ def tile_routed_moe_kernel(tc, xT, w_words, w_scales, b, gate, offs, pos1, pos2,
         quantize(1, 0, T)
         for lo, hi in PIECES:
             gather(s_scales, x_scales, lo, hi)
-        for e in range(E):
-            gather(s_words[1], x_words[1], e * C, (e + 1) * C)
+        for lo, hi in RUNS:
+            gather(s_words[1], x_words[1], lo, hi)
 
         y = [keep.tile([P, S], F32, name=name, align_bytes=64) for name in ("y0", "s_words1")]
         acc = {}
 
-        def multiply(g, e, a):
-            slots = slice(e * C, (e + 1) * C)
-            if g == 0:
-                acc[e, a] = psum.tile([P, C], F32, name=f"acc{e}_{a}")
+        def multiply(g, lo, hi, a):
+            e = lo // C
             nc.tensor.matmul_mx(
-                out=acc[e, a][:],
+                out=acc[lo, a],
                 lhsT=w_codes[:, e * G + g, a * 4 * P : (a + 1) * 4 * P].bitcast(FP8X4),
                 lhsT_scale=w_planes[:, e * G + g, a * P : (a + 1) * P],
-                rhs=s_words[g][:, slots].bitcast(FP8X4),
-                rhs_scale=s_scales[4 * g : P, slots],
+                rhs=s_words[g][:, lo:hi].bitcast(FP8X4),
+                rhs_scale=s_scales[4 * g : P, lo:hi],
                 start=(g == 0),
                 stop=(g == G - 1),
             )
 
-        for e in range(E):
-            for a in range(NB):
-                multiply(0, e, a)
+        early = [(run, a) for a in range(NB) for run in RUNS if run[1] - run[0] == C]
+        late = [(run, a) for a in range(NB) for run in RUNS if run[1] - run[0] < C]
+        bank = {key: n % 8 for n, key in enumerate(early + late)}
+        for (lo, hi), a in early:
+            acc[lo, a] = psum.tile([P, C], F32, name=f"acc{bank[(lo, hi), a]}")[:]
+            multiply(0, lo, hi, a)
         for a in range(NB):
-            for e in range(E):
-                multiply(1, e, a)
-                slots = slice(e * C, (e + 1) * C)
-                nc.scalar.activation(y[a][:, slots], acc[e, a][:], RELU, bias=bias[:, a, e : e + 1])
+            for lo, hi in RUNS:
+                if hi - lo < C:
+                    acc[lo, a] = psum.tile([P, hi - lo], F32, name=f"acc{bank[(lo, hi), a]}")[:]
+                    multiply(0, lo, hi, a)
+                multiply(1, lo, hi, a)
+                nc.scalar.activation(y[a][:, lo:hi], acc[lo, a], RELU, bias=bias[:, a, lo // C : lo // C + 1])
 
         first = [keep.tile([P, T], F32, name="first0"), None]
         second = [keep.tile([P, T], F32, name=f"second{a}") for a in range(NB)]
         total = [keep.tile([P, T], F32, name=f"total{a}") for a in range(NB)]
-        both = psum.tile([P, T], F32, name="acc0_0")
+        both = psum.tile([P, T], F32, name="acc2")
 
         def fetch(dst, a, r, lo, hi):
             pos_t = (pos1_t, pos2_t)[r]

from contextlib import ExitStack

import concourse.mybir as mybir
from concourse.masks import make_identity

F32 = mybir.dt.float32
BF16 = mybir.dt.bfloat16
U32 = mybir.dt.uint32
I32 = mybir.dt.int32
U16 = mybir.dt.uint16
U8 = mybir.dt.uint8
FP8X4 = mybir.dt.float8_e4m3fn_x4
RELU = mybir.ActivationFunctionType.Relu
MULT = mybir.AluOpType.mult
ADD = mybir.AluOpType.add

P = 128
K, T, E, C, N = 1024, 512, 4, 256, 256
G = K // 512
NB = N // P
S = E * C
HALF = T // 2
LOADS = (((0, 384), (384, 512)), ((0, 192), (192, 384), (384, 512)))
VEC = {0: 248, 384: 84}
BY_PE = 384
SPLIT = 320
RUNS = ((0, 256), (256, 512), (512, 768), (768, 896), (896, 1024))
PIECES = ((0, 384), (384, 768), (768, 1024))

FLOPS = 2 * K * N * S


def tile_routed_moe_kernel(tc, xT, w_words, w_scales, b, gate, offs, pos1, pos2, out):
    nc = tc.nc
    with ExitStack() as ctx:
        lists = ctx.enter_context(tc.tile_pool(name="lists", bufs=1))
        keep = ctx.enter_context(tc.tile_pool(name="keep", bufs=1))
        psum = ctx.enter_context(tc.psum_pool(name="psum", bufs=1))

        offs_t = lists.tile([P, S // 16], U16, name="offs_t")
        pos1_t = lists.tile([P, T // 16], U16, name="pos1_t")
        pos2_t = lists.tile([P, T // 16], U16, name="pos2_t")

        raw = [keep.tile([P, 4, T], F32, name=f"raw{g}") for g in range(G)]
        grouped = [keep.tile([P, T, 4], BF16, name=f"grouped{g}", align_bytes=64) for g in range(G)]
        x_words = [keep.tile([P, T], U32, name=f"x_words{g}", align_bytes=64) for g in range(G)]
        x_scales = keep.tile([P, T], U8, name="x_scales", align_bytes=64)
        s_words = [keep.tile([P, S], U32, name=f"s_words{g}", align_bytes=64) for g in range(G)]
        s_scales = keep.tile([P, S], U8, name="s_scales", align_bytes=64)
        w_codes = keep.tile([P, E * G, 4 * N], U8, name="w_codes", align_bytes=64)
        w_planes = keep.tile([P, E * G, N], U8, name="w_planes", align_bytes=64)
        bias = keep.tile([P, NB, E], F32, name="bias")
        gates = keep.tile([P, NB, 2, T], F32, name="gates")

        ident = keep.tile([P, P], F32, name="ident")
        nc.gpsimd.memset(x_scales[:], 0)
        make_identity(nc, ident[:])
        nc.vector.memset(w_planes[:].rearrange("p a n -> p (a n)").bitcast(I32), 0)

        x_view = xT.rearrange("(g p t) n -> g p t n", p=P, t=4)
        for g in range(G):
            for lo, hi in LOADS[g]:
                nc.sync.dma_start(out=raw[g][:, :, lo:hi], in_=x_view[g, :, :, lo:hi])
            if g == 0:
                nc.sync.dma_start(offs_t[:], offs)
        for q in range(4):
            nc.sync.dma_start(
                out=w_planes[32 * q : 32 * q + 4, :, :].bitcast(I32),
                in_=w_scales[:, :, 4 * q : 4 * q + 4, :].rearrange("e a i n -> i (e a) n").bitcast(I32),
            )
        w_view = w_words.rearrange("e a p n r -> p (e a) (n r)")
        for e in range(0, E, 2):
            ea = slice(e * G, (e + 2) * G)
            nc.sync.dma_start(out=w_codes[:, ea, :].bitcast(I32), in_=w_view[:, ea, :].bitcast(I32))
        nc.sync.dma_start(out=bias[:], in_=b.rearrange("(a p) e -> p a e", p=P))
        nc.sync.dma_start(pos1_t[:], pos1)
        nc.sync.dma_start(pos2_t[:], pos2)
        for a in range(NB):
            nc.sync.dma_start(out=gates[:, a, :, :], in_=gate[:, a * P : (a + 1) * P, :].rearrange("r p t -> p r t"))

        def interleave(g, lo, hi):
            mid = lo + VEC[lo] if g == 0 else lo
            for engine_copy, a, z in ((nc.vector.tensor_copy, lo, mid), (nc.scalar.copy, mid, hi)):
                if z > a:
                    engine_copy(
                        grouped[g][:, a:z, :].rearrange("p (c i) t -> p c t i", i=4),
                        raw[g][:, :, a:z].rearrange("p t (c i) -> p c t i", i=4),
                    )

        def quantize(g, lo, hi):
            cols = slice(lo, hi)
            nc.vector.quantize_mx(
                out=x_words[g][:, cols].bitcast(FP8X4),
                scales=x_scales[4 * g : P, cols],
                in_=grouped[g][:, cols, :].rearrange("p n t -> p (n t)"),
            )

        def gather(dst, src, lo, hi):
            nc.vector.tensor_copy(dst[:, lo:hi], src[:].indirect(offs_t[:, lo // 16 : hi // 16]))

        for lo, hi in LOADS[0]:
            interleave(0, lo, hi)
        quantize(0, 0, 256)
        quantize(0, 256, 384)
        quantize(0, 384, 512)
        for lo, hi in LOADS[1]:
            interleave(1, lo, hi)
        for lo, hi in PIECES:
            gather(s_words[0], x_words[0], lo, hi)
        quantize(1, 0, T)
        for lo, hi in PIECES:
            gather(s_scales, x_scales, lo, hi)
        for lo, hi in RUNS:
            gather(s_words[1], x_words[1], lo, hi)

        y = [keep.tile([P, S], F32, name=name, align_bytes=64) for name in ("y0", "s_words1")]
        acc = {}

        def multiply(g, lo, hi, a):
            e = lo // C
            nc.tensor.matmul_mx(
                out=acc[lo, a],
                lhsT=w_codes[:, e * G + g, a * 4 * P : (a + 1) * 4 * P].bitcast(FP8X4),
                lhsT_scale=w_planes[:, e * G + g, a * P : (a + 1) * P],
                rhs=s_words[g][:, lo:hi].bitcast(FP8X4),
                rhs_scale=s_scales[4 * g : P, lo:hi],
                start=(g == 0),
                stop=(g == G - 1),
            )

        early = [(run, a) for a in range(NB) for run in RUNS if run[1] - run[0] == C]
        late = [(run, a) for a in range(NB) for run in RUNS if run[1] - run[0] < C]
        bank = {key: n % 8 for n, key in enumerate(early + late)}
        for (lo, hi), a in early:
            acc[lo, a] = psum.tile([P, C], F32, name=f"acc{bank[(lo, hi), a]}")[:]
            multiply(0, lo, hi, a)
        for a in range(NB):
            for lo, hi in RUNS:
                if hi - lo < C:
                    acc[lo, a] = psum.tile([P, hi - lo], F32, name=f"acc{bank[(lo, hi), a]}")[:]
                    multiply(0, lo, hi, a)
                multiply(1, lo, hi, a)
                nc.scalar.activation(y[a][:, lo:hi], acc[lo, a], RELU, bias=bias[:, a, lo // C : lo // C + 1])

        first = [keep.tile([P, T], F32, name="first0"), None]
        second = [keep.tile([P, T], F32, name=f"second{a}") for a in range(NB)]
        total = [keep.tile([P, T], F32, name=f"total{a}") for a in range(NB)]
        both = psum.tile([P, T], F32, name="acc2")

        def fetch(dst, a, r, lo, hi):
            pos_t = (pos1_t, pos2_t)[r]
            nc.vector.tensor_tensor(dst[:, lo:hi], y[a][:].indirect(pos_t[:, lo // 16 : hi // 16]), gates[:, a, r, lo:hi], MULT)

        def add_on_vector(a, lo, hi):
            nc.vector.tensor_tensor(total[a][:, lo:hi], first[a][:, lo:hi], second[a][:, lo:hi], ADD)
            nc.sync.dma_start(out=out[a * P : (a + 1) * P, lo:hi], in_=total[a][:, lo:hi])

        fetch(first[0], 0, 0, 0, T)
        nc.tensor.matmul(both[:, :BY_PE], ident[:], first[0][:, :BY_PE], start=True, stop=False)
        fetch(second[0], 0, 1, 0, T)
        nc.tensor.matmul(both[:, :BY_PE], ident[:], second[0][:, :BY_PE], start=False, stop=True)
        nc.scalar.copy(total[0][:, :BY_PE], both[:, :BY_PE])
        nc.sync.dma_start(out=out[:P, :BY_PE], in_=total[0][:, :BY_PE])
        first[1] = keep.tile([P, T], F32, name="y0", align_bytes=64)
        fetch(first[1], 1, 0, 0, T)
        add_on_vector(0, BY_PE, T)
        for lo, hi in ((0, SPLIT), (SPLIT, T)):
            fetch(second[1], 1, 1, lo, hi)
        for lo, hi in ((0, SPLIT), (SPLIT, T)):
            add_on_vector(1, lo, hi)
